import numpy as np
import ml_dtypes


def mxq(x, axis, fmt="e4m3"):
    dtype, down = {"e4m3": (ml_dtypes.float8_e4m3fn, 7), "e5m2": (ml_dtypes.float8_e5m2, 14)}[fmt]
    v = np.moveaxis(np.asarray(x, np.float32).astype(ml_dtypes.bfloat16).astype(np.float64), axis, -1)
    blocks = v.reshape(v.shape[:-1] + (-1, 32))
    amax = np.abs(blocks).max(-1, keepdims=True)
    byte = np.maximum(np.where(amax > 0, np.frexp(amax)[1] - 1 + 127, 0) - down, 1)
    scale = np.exp2(byte - 127.0)
    codes = (blocks / scale).astype(np.float32).astype(dtype).astype(np.float64)
    return np.moveaxis((codes * scale).reshape(v.shape), -1, axis)


WIDE = False


def mx_kscale(k):
    if not WIDE:
        return np.ones(k)
    levels = np.array([10, -10, 5, -5, 0])
    if k % 512:
        return np.exp2(np.random.permutation(np.resize(levels, k // 32))).repeat(32)
    a = np.empty((k // 512, 16))
    for p in range(k // 512):
        a[p, :8] = np.random.permutation(np.resize(levels, 8))
        for g in range(8):
            far = levels[np.abs(levels - a[p, g]) >= 10]
            a[p, g + 8] = far[np.random.randint(len(far))]
    return np.exp2(a.ravel()).repeat(32)


def f64(x):
    return np.asarray(x).astype(np.float64)


def striped(idx):
    return np.tile(np.asarray(idx).reshape(-1, 16).T, (8, 1)).astype(np.uint16)


def unstriped(offs):
    return offs[:16].T.reshape(-1).astype(np.int64)


E2M1 = np.array([0.0, 0.5, 1.0, 1.5, 2.0, 3.0, 4.0, 6.0, -0.0, -0.5, -1.0, -1.5, -2.0, -3.0, -4.0, -6.0])


def pack_weight(w, fmt):
    k, n = w.shape
    w = f64(np.asarray(w, np.float32).astype(ml_dtypes.bfloat16)).reshape(k // 32, 32, n)
    amax = np.abs(w).max(1)
    if fmt == "e4m3":
        byte = np.frexp(amax)[1] - 1 + 127 - 7
    else:
        mant, ex = np.frexp(amax / 6.0)
        byte = np.where(mant > 0.5, ex, ex - 1) + 127
    byte = np.clip(np.where(amax > 0, byte, 1), 1, 254)
    scaled = (w * np.exp2(127.0 - byte)[:, None, :]).reshape(k, n).astype(np.float32)
    by_word = np.ascontiguousarray(scaled.reshape(k // 512, 128, 4, n).transpose(0, 1, 3, 2))
    if fmt == "e4m3":
        words = by_word.astype(ml_dtypes.float8_e4m3fn).view(np.uint8)
    else:
        c = by_word.astype(ml_dtypes.float4_e2m1fn).view(np.uint8) & 0xF
        words = (c[..., 0::2] | (c[..., 1::2] << 4)).reshape(k // 512, 128, 2 * n)
    return np.ascontiguousarray(words), np.ascontiguousarray(byte.astype(np.uint8).reshape(k // 512, 16, n))


def unpack_weight(words, scales, fmt):
    g, _, n = scales.shape
    words = np.ascontiguousarray(words).reshape(g, 128, n, -1)
    if fmt == "e4m3":
        vals = words.view(ml_dtypes.float8_e4m3fn).astype(np.float64)
    else:
        nib = np.empty((g, 128, n, 4), np.uint8)
        nib[..., 0::2] = words & 0xF
        nib[..., 1::2] = words >> 4
        vals = E2M1[nib]
    vals = vals * np.repeat(np.exp2(scales.astype(np.float64) - 127.0), 8, axis=1)[..., None]
    return vals.transpose(0, 1, 3, 2).reshape(g * 512, n)


B, N, T, D, DV, NQ = 2, 1024, 4096, 512, 256, 128
PAGE = 512
CAP = 2.0


def setup_inputs():
    n = np.random.standard_normal
    pages = np.random.permutation(T // PAGE)[:B * N // PAGE]
    idx = (pages[:, None] * PAGE + np.arange(PAGE)[None, :]).reshape(-1)
    s = mx_kscale(D)[:, None]
    u = np.ones(T)
    u[idx] = mx_kscale(B * N)
    r = np.random.uniform(0.5, 2.0, T)
    k = n((D, T)) / s
    v = n((DV, T)) / (u * r)
    kp = pack_weight(k, "e4m3")
    vp = pack_weight(v.T, "e4m3")
    return {
        "qT": (n((B, D, NQ)) * s * (1.00 / np.sqrt(D))).astype(np.float32),
        "k_words": kp[0],
        "k_scales": kp[1],
        "v_words": vp[0],
        "v_scales": vp[1],
        "vs": np.tile(u * r, (128, 1)).astype(np.float32),
        "kb": np.tile(n(T), (128, 1)).astype(np.float32),
        "offs": striped(idx),
        "voffs": striped((pages[:, None] * DV + np.arange(DV)[None, :]).reshape(-1)),
    }


def reference(qT, k_words, k_scales, v_words, v_scales, vs, kb, offs, voffs):
    idx = unstriped(offs)
    k = unpack_weight(k_words, k_scales, "e4m3")
    v = unpack_weight(v_words, v_scales, "e4m3")
    v = v.reshape(T // 512, 512, DV)[unstriped(voffs)[::DV] // DV].reshape(B, N, DV)
    pick = lambda x: x[:, idx].reshape(x.shape[0], B, N).transpose(1, 0, 2)
    q = f64(qT)
    score = mxq(q, 1, "e4m3").transpose(0, 2, 1) @ pick(k)
    score = score + pick(f64(kb))[:, :1, :]
    score = CAP * np.tanh(score / CAP)
    m = score.max(-1, keepdims=True)
    p = np.exp(score - m)
    total = p.sum(-1, keepdims=True)
    w = p * pick(f64(vs))[:, :1, :]
    y = mxq(w, 2, "e4m3") @ v
    y = y / total
    return y

@@ -1,0 +1,247 @@
+from contextlib import ExitStack
+
+import concourse.mybir as mybir
+from concourse.masks import make_identity
+
+B, N, T, D, DV, NQ = 2, 1024, 4096, 512, 256, 128
+PAGE = 512
+CAP = 2.0
+
+F32 = mybir.dt.float32
+BF16 = mybir.dt.bfloat16
+I32 = mybir.dt.int32
+U32 = mybir.dt.uint32
+U16 = mybir.dt.uint16
+U8 = mybir.dt.uint8
+FP8X4 = mybir.dt.float8_e4m3fn_x4
+ACT = mybir.ActivationFunctionType
+ALU = mybir.AluOpType
+
+P = 128
+PACK = 4
+LIST_ROWS = 16
+PAGES = N // PAGE
+POOL_PAGES = T // PAGE
+TILES = PAGE // P
+
+FLOPS = 2 * B * NQ * N * (D + DV)
+BYTES = 4 * B * D * NQ + T * D + T * D // 32 + T * DV + T * DV // 32 + 2 * 4 * T + 2 * P * (B * N + B * PAGES * DV) // 16 + 4 * B * NQ * DV
+
+
+def tile_attend_pkv8_soft_cap_kb_kernel(
+    tc, qT, k_words, k_scales, v_words, v_scales, vs, kb, offs, voffs, out
+):
+    nc = tc.nc
+    with ExitStack() as ctx:
+        held = ctx.enter_context(tc.tile_pool(name="held", bufs=1))
+        psum = ctx.enter_context(tc.psum_pool(name="psum", bufs=1))
+
+        def sb(shape, dtype, name, tag=None):
+            return held.tile(shape, dtype, name=name, tag=tag or name, align_bytes=64)
+
+        def bank(tag):
+            return psum.tile([P, TILES, P], F32, name=tag, tag=tag, bufs={"score_bank": 2, "turn_bank": 5}[tag])
+
+        slots = held.tile([P, B * N // LIST_ROWS], U16, name="slots")
+        vcols = held.tile([P, B * PAGES * DV // LIST_ROWS], U16, name="vcols")
+        nc.sync.dma_start(slots[:], offs)
+
+        def listed(lst, start, count):
+            return lst[:, start // LIST_ROWS : (start + count) // LIST_ROWS]
+
+        nc.sync.dma_start(vcols[:], voffs)
+        k_byte_pool = sb([P, T], U8, "k_byte_pool")
+        nc.vector.memset(k_byte_pool[:].bitcast(I32), 0)
+        for quad in range(4):
+            nc.sync.dma_start(
+                k_byte_pool[32 * quad : 32 * quad + 4, :].bitcast(I32),
+                k_scales[0, 4 * quad : 4 * quad + 4, :].bitcast(I32),
+            )
+        kb_pool = sb([P, T], F32, "kb_pool")
+        nc.vector.memset(kb_pool[:].bitcast(I32), 0)
+        identity = sb([P, P], F32, "identity")
+        make_identity(nc, identity[:])
+        nc.scalar.dma_start(kb_pool[0:1, :], kb[0:1, :])
+        v_byte_pool = sb([P, POOL_PAGES * DV], U8, "v_byte_pool")
+        nc.gpsimd.memset(v_byte_pool[:].bitcast(I32), 0)
+
+        q_raw = sb([P, B, PACK, NQ], F32, "q_raw")
+        nc.sync.dma_start(
+            q_raw[:].rearrange("p b j q -> p b (j q)"), qT.rearrange("b (p j) q -> p b (j q)", j=PACK)
+        )
+        k_word_pool = sb([P, T], I32, "k_word_pool")
+        nc.sync.dma_start(k_word_pool[:], k_words[0].rearrange("p t r -> p (t r)").bitcast(I32))
+
+        q_woven = sb([P, B, NQ, PACK], BF16, "q_woven")
+        nc.scalar.copy(q_woven[:], q_raw[:].rearrange("p b j q -> p b q j"))
+        q_codes = sb([P, B * NQ], U32, "q_codes")
+        q_bytes = sb([P, B * NQ], U8, "q_bytes")
+
+        def columns(row_tile_of, name, scale, tag):
+            turned = bank(tag)
+            for j in range(TILES):
+                nc.tensor.transpose(turned[:, j, :], row_tile_of(j), identity[:])
+            cols = sb([P, TILES], F32, name)
+            nc.scalar.activation(cols[:], turned[:, :, 0], ACT.Copy, scale=scale)
+            return cols
+
+        k_bytes, half_kb, capped, neg_c, neg_m, probs, sums, vs_cols, woven = {}, {}, {}, {}, {}, {}, {}, {}, {}
+
+        def gather_key_bytes(b):
+            k_bytes[b] = sb([P, N], U8, f"k_bytes{b}")
+            nc.vector.tensor_copy(k_bytes[b][:], k_byte_pool[:].indirect(listed(slots, b * N, N)))
+
+        def gather_bias(b):
+            row = sb([P, N], F32, f"kb_row{b}")
+            nc.vector.tensor_copy(row[:], kb_pool[:].indirect(listed(slots, b * N, N)))
+            for g in range(PAGES):
+                half_kb[b, g] = columns(
+                    lambda j: row[:, g * PAGE + j * P : g * PAGE + (j + 1) * P], f"half_kb{b}{g}", 1.0 / CAP, "turn_bank"
+                )
+
+        def scores(b, g):
+            words = sb([P, PAGE], U32, f"k_words{b}{g}")
+            nc.vector.tensor_copy(
+                words[:], k_word_pool[:].bitcast(U32).indirect(listed(slots, b * N + g * PAGE, PAGE))
+            )
+            acc = bank("score_bank")
+            for j in range(TILES):
+                nc.tensor.matmul_mx(
+                    out=acc[:, j, :],
+                    lhsT=words[:, j * P : (j + 1) * P].bitcast(FP8X4),
+                    lhsT_scale=k_bytes[b][:, g * PAGE + j * P : g * PAGE + (j + 1) * P],
+                    rhs=q_codes[:, b * NQ : (b + 1) * NQ].bitcast(FP8X4),
+                    rhs_scale=q_bytes[:, b * NQ : (b + 1) * NQ],
+                    start=True,
+                    stop=True,
+                )
+            th = sb([P, TILES, NQ], F32, f"tanh{b}{g}")
+            for j in range(TILES):
+                nc.scalar.activation(
+                    th[:, j, :], acc[:, j, :], ACT.Tanh, bias=half_kb[b, g][:, j : j + 1], scale=1.0 / CAP
+                )
+            capped[b, g] = bank("turn_bank")
+            for j in range(TILES):
+                nc.tensor.transpose(capped[b, g][:, j, :], th[:, j, :], identity[:])
+
+        def row_maximum(b, g):
+            neg_c[b, g] = sb([P, PACK, P], F32, f"neg_c{b}{g}")
+            neg_m[b, g] = sb([P, 1], F32, f"neg_m{b}{g}")
+            nc.vector.tensor_scalar(
+                neg_c[b, g][:],
+                capped[b, g][:].rearrange("q j s -> q (j s)").rearrange("q (s r) -> q r s", r=PACK),
+                -CAP,
+                neg_m[b, g - 1][:] if g else None,
+                ALU.mult,
+                ALU.min,
+                accum_out=neg_m[b, g][:],
+            )
+
+        def exponentials(b, g):
+            th = sb([P, PACK, P], F32, f"p{b}{g}")
+            sums[b, g] = sb([P, 1], F32, f"l{b}{g}")
+            nc.scalar.activation(
+                th[:], neg_c[b, g][:], ACT.Exp, bias=neg_m[b, PAGES - 1][:], scale=-1.0, accum_out=sums[b, g][:]
+            )
+            probs[b, g] = bank("turn_bank")
+            for r in range(PACK):
+                nc.tensor.transpose(probs[b, g][:, r, :], th[:, r, :], identity[:])
+
+        def gather_token_scales(b):
+            row = sb([P, N], F32, f"vs_row{b}", tag=f"tanh{B - 1}{b}")
+            nc.vector.tensor_copy(row[:], vs_pool[:].indirect(listed(slots, b * N, N)))
+            return row
+
+        def token_scale_columns(b, row):
+            for g in range(PAGES):
+                vs_cols[b, g] = columns(
+                    lambda r: row[:, g * PAGE + r : (g + 1) * PAGE : PACK], f"vs_cols{b}{g}", 1.0, "score_bank"
+                )
+
+        def weigh(b, g):
+            flat = sb([P, PACK, NQ], BF16, f"w_flat{b}{g}")
+            for r in range(PACK):
+                nc.scalar.activation(flat[:, r, :], probs[b, g][:, r, :], ACT.Copy, scale=vs_cols[b, g][:, r : r + 1])
+            woven[b, g] = sb([P, NQ, PACK], BF16, f"w_woven{b}{g}")
+            nc.scalar.copy(
+                woven[b, g][:].rearrange("p (c i) r -> p c r i", i=4),
+                flat[:].rearrange("p r (c i) -> p c r i", i=4),
+            )
+
+        v_codes = {}
+
+        def gather_values(b, word_tag):
+            picked = listed(vcols, b * PAGES * DV, PAGES * DV)
+            v_codes[b] = sb([P, PAGES * DV], U32, f"v_codes{b}", tag=word_tag)
+            nc.vector.tensor_copy(v_codes[b][:], v_word_pool[:].bitcast(U32).indirect(picked))
+
+        out_bank = psum.tile([P, B, DV], F32, name="out_bank")
+
+        def finish(b):
+            total = sb([P, 1], F32, f"total{b}")
+            nc.scalar.activation(total[:], sums[b, 0][:], ACT.Identity, bias=sums[b, 1][:], scale=1.0)
+            inverse = sb([P, 1], F32, f"inverse{b}")
+            nc.vector.reciprocal(inverse[:], total[:])
+            for g in range(PAGES):
+                w_codes = sb([P, NQ], U32, f"w_codes{b}{g}")
+                w_bytes = sb([P, NQ], U8, f"w_bytes{b}{g}")
+                nc.vector.quantize_mx(
+                    out=w_codes[:].bitcast(FP8X4), scales=w_bytes[:], in_=woven[b, g][:].rearrange("p q r -> p (q r)")
+                )
+                nc.tensor.matmul_mx(
+                    out=out_bank[:, b, :],
+                    lhsT=w_codes[:].bitcast(FP8X4),
+                    lhsT_scale=w_bytes[:],
+                    rhs=v_codes[b][:, g * DV : (g + 1) * DV].bitcast(FP8X4),
+                    rhs_scale=v_bytes[:, (b * PAGES + g) * DV : (b * PAGES + g + 1) * DV],
+                    start=(g == 0),
+                    stop=(g == PAGES - 1),
+                )
+            result = sb([P, DV], F32, f"result{b}")
+            nc.scalar.activation(result[:], out_bank[:, b, :], ACT.Copy, scale=inverse[:])
+            nc.sync.dma_start(out[b], result[:])
+
+        for b in range(B):
+            gather_key_bytes(b)
+        nc.vector.quantize_mx(
+            out=q_codes[:].bitcast(FP8X4), scales=q_bytes[:], in_=q_woven[:].rearrange("p b q j -> p (b q j)")
+        )
+        vs_pool = sb([P, T], F32, "vs_pool", tag="q_woven")
+        nc.sync.dma_start(vs_pool[:], vs)
+        v_word_pool = sb([P, POOL_PAGES * DV], I32, "v_word_pool", tag="q_raw")
+        nc.sync.dma_start(
+            v_word_pool[:].rearrange("p (u e) -> p u e", u=POOL_PAGES),
+            v_words.rearrange("u p e r -> p u (e r)").bitcast(I32),
+        )
+        for quad in range(4):
+            nc.sync.dma_start(
+                v_byte_pool[32 * quad : 32 * quad + 4, :].bitcast(I32).rearrange("f (u e) -> f u e", u=POOL_PAGES),
+                v_scales[:, 4 * quad : 4 * quad + 4, :].rearrange("u f e -> f u e").bitcast(I32),
+            )
+
+        for b in range(B):
+            gather_bias(b)
+        for b in range(B):
+            for g in range(PAGES):
+                scores(b, g)
+        for g in range(PAGES):
+            row_maximum(0, g)
+        for g in range(PAGES):
+            exponentials(0, g)
+        token_scale_columns(0, gather_token_scales(0))
+        for g in range(PAGES):
+            row_maximum(1, g)
+        for g in range(PAGES):
+            exponentials(1, g)
+        vs_row = gather_token_scales(1)
+        for g in range(PAGES):
+            weigh(0, g)
+        token_scale_columns(1, vs_row)
+        for g in range(PAGES):
+            weigh(1, g)
+        v_bytes = sb([P, B * PAGES * DV], U8, "v_bytes", tag="neg_c10")
+        nc.vector.tensor_copy(v_bytes[:], v_byte_pool[:].indirect(vcols[:]))
+        gather_values(0, "neg_c11")
+        gather_values(1, "p11")
+        for b in range(B):
+            finish(b)

@@ -40,7 +40,7 @@ def tile_attend_pkv8_soft_cap_kb_kernel(
             return held.tile(shape, dtype, name=name, tag=tag or name, align_bytes=64)
 
         def bank(tag):
-            return psum.tile([P, TILES, P], F32, name=tag, tag=tag, bufs={"score_bank": 2, "turn_bank": 5}[tag])
+            return psum.tile([P, TILES, P], F32, name=tag, tag=tag, bufs={"score_bank": 2, "spare_bank": 2, "turn_bank": 4}[tag])
 
         slots = held.tile([P, B * N // LIST_ROWS], U16, name="slots")
         vcols = held.tile([P, B * PAGES * DV // LIST_ROWS], U16, name="vcols")
@@ -52,11 +52,7 @@ def tile_attend_pkv8_soft_cap_kb_kernel(
         nc.sync.dma_start(vcols[:], voffs)
         k_byte_pool = sb([P, T], U8, "k_byte_pool")
         nc.vector.memset(k_byte_pool[:].bitcast(I32), 0)
-        for quad in range(4):
-            nc.sync.dma_start(
-                k_byte_pool[32 * quad : 32 * quad + 4, :].bitcast(I32),
-                k_scales[0, 4 * quad : 4 * quad + 4, :].bitcast(I32),
-            )
+        nc.scalar.dma_start(k_byte_pool[0:P:8, :].bitcast(I32), k_scales[0].bitcast(I32))
         kb_pool = sb([P, T], F32, "kb_pool")
         nc.vector.memset(kb_pool[:].bitcast(I32), 0)
         identity = sb([P, P], F32, "identity")
@@ -64,6 +60,8 @@ def tile_attend_pkv8_soft_cap_kb_kernel(
         nc.scalar.dma_start(kb_pool[0:1, :], kb[0:1, :])
         v_byte_pool = sb([P, POOL_PAGES * DV], U8, "v_byte_pool")
         nc.gpsimd.memset(v_byte_pool[:].bitcast(I32), 0)
+        k_plane = sb([P, B * N], U8, "k_plane")
+        nc.gpsimd.memset(k_plane[:].bitcast(I32), 0)
 
         q_raw = sb([P, B, PACK, NQ], F32, "q_raw")
         nc.sync.dma_start(
@@ -77,39 +75,41 @@ def tile_attend_pkv8_soft_cap_kb_kernel(
         q_codes = sb([P, B * NQ], U32, "q_codes")
         q_bytes = sb([P, B * NQ], U8, "q_bytes")
 
-        def columns(row_tile_of, name, scale, tag):
+        def columns(row_tile_of, name, scale, tag, cols_tag=None):
             turned = bank(tag)
             for j in range(TILES):
                 nc.tensor.transpose(turned[:, j, :], row_tile_of(j), identity[:])
-            cols = sb([P, TILES], F32, name)
+            cols = sb([P, TILES], F32, name, tag=cols_tag)
             nc.scalar.activation(cols[:], turned[:, :, 0], ACT.Copy, scale=scale)
             return cols
 
-        k_bytes, half_kb, capped, neg_c, neg_m, probs, sums, vs_cols, woven = {}, {}, {}, {}, {}, {}, {}, {}, {}
+        half_kb, capped, neg_c, neg_m, probs, sums, vs_cols, woven = {}, {}, {}, {}, {}, {}, {}, {}
 
-        def gather_key_bytes(b):
-            k_bytes[b] = sb([P, N], U8, f"k_bytes{b}")
-            nc.vector.tensor_copy(k_bytes[b][:], k_byte_pool[:].indirect(listed(slots, b * N, N)))
+        def gather_key_bytes():
+            k_bytes = sb([P, B * N], U8, "k_bytes")
+            nc.vector.tensor_copy(k_bytes[:], k_byte_pool[:].indirect(slots[:]))
+            for j in range(4):
+                nc.sync.dma_start(k_plane[j:P:32, :].bitcast(I32), k_bytes[8 * j : P : 32, :].bitcast(I32))
 
         def gather_bias(b):
             row = sb([P, N], F32, f"kb_row{b}")
             nc.vector.tensor_copy(row[:], kb_pool[:].indirect(listed(slots, b * N, N)))
             for g in range(PAGES):
                 half_kb[b, g] = columns(
-                    lambda j: row[:, g * PAGE + j * P : g * PAGE + (j + 1) * P], f"half_kb{b}{g}", 1.0 / CAP, "turn_bank"
+                    lambda j: row[:, g * PAGE + j * P : g * PAGE + (j + 1) * P], f"half_kb{b}{g}", 1.0 / CAP, "spare_bank"
                 )
 
         def scores(b, g):
-            words = sb([P, PAGE], U32, f"k_words{b}{g}")
+            words = k_codes[:, b * PAGES + g, :]
             nc.vector.tensor_copy(
-                words[:], k_word_pool[:].bitcast(U32).indirect(listed(slots, b * N + g * PAGE, PAGE))
+                words, k_word_pool[:].bitcast(U32).indirect(listed(slots, b * N + g * PAGE, PAGE))
             )
             acc = bank("score_bank")
             for j in range(TILES):
                 nc.tensor.matmul_mx(
                     out=acc[:, j, :],
                     lhsT=words[:, j * P : (j + 1) * P].bitcast(FP8X4),
-                    lhsT_scale=k_bytes[b][:, g * PAGE + j * P : g * PAGE + (j + 1) * P],
+                    lhsT_scale=k_plane[:, b * N + g * PAGE + j * P : b * N + g * PAGE + (j + 1) * P],
                     rhs=q_codes[:, b * NQ : (b + 1) * NQ].bitcast(FP8X4),
                     rhs_scale=q_bytes[:, b * NQ : (b + 1) * NQ],
                     start=True,
@@ -143,19 +143,19 @@ def tile_attend_pkv8_soft_cap_kb_kernel(
             nc.scalar.activation(
                 th[:], neg_c[b, g][:], ACT.Exp, bias=neg_m[b, PAGES - 1][:], scale=-1.0, accum_out=sums[b, g][:]
             )
-            probs[b, g] = bank("turn_bank")
+            probs[b, g] = bank(("spare_bank", "turn_bank")[b])
             for r in range(PACK):
                 nc.tensor.transpose(probs[b, g][:, r, :], th[:, r, :], identity[:])
 
         def gather_token_scales(b):
-            row = sb([P, N], F32, f"vs_row{b}", tag=f"tanh{B - 1}{b}")
+            row = sb([P, N], F32, f"vs_row{b}", tag=("tanh01", "p01")[b])
             nc.vector.tensor_copy(row[:], vs_pool[:].indirect(listed(slots, b * N, N)))
             return row
 
         def token_scale_columns(b, row):
             for g in range(PAGES):
                 vs_cols[b, g] = columns(
-                    lambda r: row[:, g * PAGE + r : (g + 1) * PAGE : PACK], f"vs_cols{b}{g}", 1.0, "score_bank"
+                    lambda r: row[:, g * PAGE + r : (g + 1) * PAGE : PACK], f"vs_cols{b}{g}", 1.0, ("score_bank", "spare_bank")[b], f"vs_cols{g}"
                 )
 
         def weigh(b, g):
@@ -168,59 +168,60 @@ def tile_attend_pkv8_soft_cap_kb_kernel(
                 flat[:].rearrange("p r (c i) -> p c r i", i=4),
             )
 
-        v_codes = {}
+        def gather_values(first, count, tag):
+            codes = sb([P, count * DV], U32, f"v_codes{first}", tag=tag)
+            nc.vector.tensor_copy(codes[:], v_word_pool[:].bitcast(U32).indirect(listed(vcols, first * DV, count * DV)))
+            return [codes[:, n * DV : (n + 1) * DV] for n in range(count)]
 
-        def gather_values(b, word_tag):
-            picked = listed(vcols, b * PAGES * DV, PAGES * DV)
-            v_codes[b] = sb([P, PAGES * DV], U32, f"v_codes{b}", tag=word_tag)
-            nc.vector.tensor_copy(v_codes[b][:], v_word_pool[:].bitcast(U32).indirect(picked))
+        inverse = {}
 
-        out_bank = psum.tile([P, B, DV], F32, name="out_bank")
-
-        def finish(b):
+        def row_sums(b):
             total = sb([P, 1], F32, f"total{b}")
             nc.scalar.activation(total[:], sums[b, 0][:], ACT.Identity, bias=sums[b, 1][:], scale=1.0)
-            inverse = sb([P, 1], F32, f"inverse{b}")
-            nc.vector.reciprocal(inverse[:], total[:])
-            for g in range(PAGES):
-                w_codes = sb([P, NQ], U32, f"w_codes{b}{g}")
-                w_bytes = sb([P, NQ], U8, f"w_bytes{b}{g}")
-                nc.vector.quantize_mx(
-                    out=w_codes[:].bitcast(FP8X4), scales=w_bytes[:], in_=woven[b, g][:].rearrange("p q r -> p (q r)")
-                )
-                nc.tensor.matmul_mx(
-                    out=out_bank[:, b, :],
-                    lhsT=w_codes[:].bitcast(FP8X4),
-                    lhsT_scale=w_bytes[:],
-                    rhs=v_codes[b][:, g * DV : (g + 1) * DV].bitcast(FP8X4),
-                    rhs_scale=v_bytes[:, (b * PAGES + g) * DV : (b * PAGES + g + 1) * DV],
-                    start=(g == 0),
-                    stop=(g == PAGES - 1),
-                )
-            result = sb([P, DV], F32, f"result{b}")
-            nc.scalar.activation(result[:], out_bank[:, b, :], ACT.Copy, scale=inverse[:])
+            inverse[b] = sb([P, 1], F32, f"inverse{b}")
+            nc.vector.reciprocal(inverse[b][:], total[:])
+
+        def multiply(b, g, acc, v_codes):
+            w_codes = sb([P, NQ], U32, f"w_codes{b}{g}")
+            w_bytes = sb([P, NQ], U8, f"w_bytes{b}{g}")
+            nc.vector.quantize_mx(
+                out=w_codes[:].bitcast(FP8X4), scales=w_bytes[:], in_=woven[b, g][:].rearrange("p q r -> p (q r)")
+            )
+            nc.tensor.matmul_mx(
+                out=acc,
+                lhsT=w_codes[:].bitcast(FP8X4),
+                lhsT_scale=w_bytes[:],
+                rhs=v_codes.bitcast(FP8X4),
+                rhs_scale=v_bytes[:, (b * PAGES + g) * DV : (b * PAGES + g + 1) * DV],
+                start=(g == 0),
+                stop=(g == PAGES - 1),
+            )
+
+        def finish(b, acc):
+            result = sb([P, DV], F32, f"result{b}", tag=f"w_flat1{1 - b}")
+            nc.scalar.activation(result[:], acc, ACT.Copy, scale=inverse[b][:])
             nc.sync.dma_start(out[b], result[:])
 
-        for b in range(B):
-            gather_key_bytes(b)
+        gather_key_bytes()
         nc.vector.quantize_mx(
             out=q_codes[:].bitcast(FP8X4), scales=q_bytes[:], in_=q_woven[:].rearrange("p b q j -> p (b q j)")
         )
-        vs_pool = sb([P, T], F32, "vs_pool", tag="q_woven")
+        vs_pool = sb([P, T], F32, "vs_pool", tag="q_raw")
         nc.sync.dma_start(vs_pool[:], vs)
-        v_word_pool = sb([P, POOL_PAGES * DV], I32, "v_word_pool", tag="q_raw")
+        v_word_pool = sb([P, POOL_PAGES * DV], I32, "v_word_pool", tag="q_woven")
         nc.sync.dma_start(
             v_word_pool[:].rearrange("p (u e) -> p u e", u=POOL_PAGES),
             v_words.rearrange("u p e r -> p u (e r)").bitcast(I32),
         )
-        for quad in range(4):
+        for j in range(4):
             nc.sync.dma_start(
-                v_byte_pool[32 * quad : 32 * quad + 4, :].bitcast(I32).rearrange("f (u e) -> f u e", u=POOL_PAGES),
-                v_scales[:, 4 * quad : 4 * quad + 4, :].rearrange("u f e -> f u e").bitcast(I32),
+                v_byte_pool[j:P:32, :].bitcast(I32).rearrange("f (u e) -> f u e", u=POOL_PAGES),
+                v_scales[:, j:16:4, :].rearrange("u f e -> f u e").bitcast(I32),
             )
 
         for b in range(B):
             gather_bias(b)
+        k_codes = sb([P, B * PAGES, PAGE], U32, "k_codes", tag="kb_row0")
         for b in range(B):
             for g in range(PAGES):
                 scores(b, g)
@@ -228,11 +229,13 @@ def tile_attend_pkv8_soft_cap_kb_kernel(
             row_maximum(0, g)
         for g in range(PAGES):
             exponentials(0, g)
+        row_sums(0)
         token_scale_columns(0, gather_token_scales(0))
         for g in range(PAGES):
             row_maximum(1, g)
         for g in range(PAGES):
             exponentials(1, g)
+        row_sums(1)
         vs_row = gather_token_scales(1)
         for g in range(PAGES):
             weigh(0, g)
@@ -241,7 +244,10 @@ def tile_attend_pkv8_soft_cap_kb_kernel(
             weigh(1, g)
         v_bytes = sb([P, B * PAGES * DV], U8, "v_bytes", tag="neg_c10")
         nc.vector.tensor_copy(v_bytes[:], v_byte_pool[:].indirect(vcols[:]))
-        gather_values(0, "neg_c11")
-        gather_values(1, "p11")
+        accs = [bank("turn_bank")[:].rearrange("q j s -> q (j s)")[:, :DV] for b in range(B)]
+        for g, v_codes in enumerate(gather_values(0, PAGES, "neg_c11")):
+            multiply(0, g, accs[0], v_codes)
+        for g, tag in enumerate(("w_flat01", "w_flat10")):
+            multiply(1, g, accs[1], gather_values(PAGES + g, 1, tag)[0])
         for b in range(B):
-            finish(b)
+            finish(b, accs[b])

from contextlib import ExitStack

import concourse.mybir as mybir
from concourse.masks import make_identity

B, N, T, D, DV, NQ = 2, 1024, 4096, 512, 256, 128
PAGE = 512
CAP = 2.0

F32 = mybir.dt.float32
BF16 = mybir.dt.bfloat16
I32 = mybir.dt.int32
U32 = mybir.dt.uint32
U16 = mybir.dt.uint16
U8 = mybir.dt.uint8
FP8X4 = mybir.dt.float8_e4m3fn_x4
ACT = mybir.ActivationFunctionType
ALU = mybir.AluOpType

P = 128
PACK = 4
LIST_ROWS = 16
PAGES = N // PAGE
POOL_PAGES = T // PAGE
TILES = PAGE // P

FLOPS = 2 * B * NQ * N * (D + DV)
BYTES = 4 * B * D * NQ + T * D + T * D // 32 + T * DV + T * DV // 32 + 2 * 4 * T + 2 * P * (B * N + B * PAGES * DV) // 16 + 4 * B * NQ * DV


def tile_attend_pkv8_soft_cap_kb_kernel(
    tc, qT, k_words, k_scales, v_words, v_scales, vs, kb, offs, voffs, out
):
    nc = tc.nc
    with ExitStack() as ctx:
        held = ctx.enter_context(tc.tile_pool(name="held", bufs=1))
        psum = ctx.enter_context(tc.psum_pool(name="psum", bufs=1))

        def sb(shape, dtype, name, tag=None):
            return held.tile(shape, dtype, name=name, tag=tag or name, align_bytes=64)

        def bank(tag):
            return psum.tile([P, TILES, P], F32, name=tag, tag=tag, bufs={"score_bank": 2, "spare_bank": 2, "turn_bank": 4}[tag])

        slots = held.tile([P, B * N // LIST_ROWS], U16, name="slots")
        vcols = held.tile([P, B * PAGES * DV // LIST_ROWS], U16, name="vcols")
        nc.sync.dma_start(slots[:], offs)

        def listed(lst, start, count):
            return lst[:, start // LIST_ROWS : (start + count) // LIST_ROWS]

        nc.sync.dma_start(vcols[:], voffs)
        k_byte_pool = sb([P, T], U8, "k_byte_pool")
        nc.vector.memset(k_byte_pool[:].bitcast(I32), 0)
        nc.scalar.dma_start(k_byte_pool[0:P:8, :].bitcast(I32), k_scales[0].bitcast(I32))
        kb_pool = sb([P, T], F32, "kb_pool")
        nc.vector.memset(kb_pool[:].bitcast(I32), 0)
        identity = sb([P, P], F32, "identity")
        make_identity(nc, identity[:])
        nc.scalar.dma_start(kb_pool[0:1, :], kb[0:1, :])
        v_byte_pool = sb([P, POOL_PAGES * DV], U8, "v_byte_pool")
        nc.gpsimd.memset(v_byte_pool[:].bitcast(I32), 0)
        k_plane = sb([P, B * N], U8, "k_plane")
        nc.gpsimd.memset(k_plane[:].bitcast(I32), 0)

        q_raw = sb([P, B, PACK, NQ], F32, "q_raw")
        nc.sync.dma_start(
            q_raw[:].rearrange("p b j q -> p b (j q)"), qT.rearrange("b (p j) q -> p b (j q)", j=PACK)
        )
        k_word_pool = sb([P, T], I32, "k_word_pool")
        nc.sync.dma_start(k_word_pool[:], k_words[0].rearrange("p t r -> p (t r)").bitcast(I32))

        q_woven = sb([P, B, NQ, PACK], BF16, "q_woven")
        nc.scalar.copy(q_woven[:], q_raw[:].rearrange("p b j q -> p b q j"))
        q_codes = sb([P, B * NQ], U32, "q_codes")
        q_bytes = sb([P, B * NQ], U8, "q_bytes")

        def columns(row_tile_of, name, scale, tag, cols_tag=None):
            turned = bank(tag)
            for j in range(TILES):
                nc.tensor.transpose(turned[:, j, :], row_tile_of(j), identity[:])
            cols = sb([P, TILES], F32, name, tag=cols_tag)
            nc.scalar.activation(cols[:], turned[:, :, 0], ACT.Copy, scale=scale)
            return cols

        half_kb, capped, neg_c, neg_m, probs, sums, vs_cols, woven = {}, {}, {}, {}, {}, {}, {}, {}

        def gather_key_bytes():
            k_bytes = sb([P, B * N], U8, "k_bytes")
            nc.vector.tensor_copy(k_bytes[:], k_byte_pool[:].indirect(slots[:]))
            for j in range(4):
                nc.sync.dma_start(k_plane[j:P:32, :].bitcast(I32), k_bytes[8 * j : P : 32, :].bitcast(I32))

        def gather_bias(b):
            row = sb([P, N], F32, f"kb_row{b}")
            nc.vector.tensor_copy(row[:], kb_pool[:].indirect(listed(slots, b * N, N)))
            for g in range(PAGES):
                half_kb[b, g] = columns(
                    lambda j: row[:, g * PAGE + j * P : g * PAGE + (j + 1) * P], f"half_kb{b}{g}", 1.0 / CAP, "spare_bank"
                )

        def scores(b, g):
            words = k_codes[:, b * PAGES + g, :]
            nc.vector.tensor_copy(
                words, k_word_pool[:].bitcast(U32).indirect(listed(slots, b * N + g * PAGE, PAGE))
            )
            acc = bank("score_bank")
            for j in range(TILES):
                nc.tensor.matmul_mx(
                    out=acc[:, j, :],
                    lhsT=words[:, j * P : (j + 1) * P].bitcast(FP8X4),
                    lhsT_scale=k_plane[:, b * N + g * PAGE + j * P : b * N + g * PAGE + (j + 1) * P],
                    rhs=q_codes[:, b * NQ : (b + 1) * NQ].bitcast(FP8X4),
                    rhs_scale=q_bytes[:, b * NQ : (b + 1) * NQ],
                    start=True,
                    stop=True,
                )
            th = sb([P, TILES, NQ], F32, f"tanh{b}{g}")
            for j in range(TILES):
                nc.scalar.activation(
                    th[:, j, :], acc[:, j, :], ACT.Tanh, bias=half_kb[b, g][:, j : j + 1], scale=1.0 / CAP
                )
            capped[b, g] = bank("turn_bank")
            for j in range(TILES):
                nc.tensor.transpose(capped[b, g][:, j, :], th[:, j, :], identity[:])

        def row_maximum(b, g):
            neg_c[b, g] = sb([P, PACK, P], F32, f"neg_c{b}{g}")
            neg_m[b, g] = sb([P, 1], F32, f"neg_m{b}{g}")
            nc.vector.tensor_scalar(
                neg_c[b, g][:],
                capped[b, g][:].rearrange("q j s -> q (j s)").rearrange("q (s r) -> q r s", r=PACK),
                -CAP,
                neg_m[b, g - 1][:] if g else None,
                ALU.mult,
                ALU.min,
                accum_out=neg_m[b, g][:],
            )

        def exponentials(b, g):
            th = sb([P, PACK, P], F32, f"p{b}{g}")
            sums[b, g] = sb([P, 1], F32, f"l{b}{g}")
            nc.scalar.activation(
                th[:], neg_c[b, g][:], ACT.Exp, bias=neg_m[b, PAGES - 1][:], scale=-1.0, accum_out=sums[b, g][:]
            )
            probs[b, g] = bank(("spare_bank", "turn_bank")[b])
            for r in range(PACK):
                nc.tensor.transpose(probs[b, g][:, r, :], th[:, r, :], identity[:])

        def gather_token_scales(b):
            row = sb([P, N], F32, f"vs_row{b}", tag=("tanh01", "p01")[b])
            nc.vector.tensor_copy(row[:], vs_pool[:].indirect(listed(slots, b * N, N)))
            return row

        def token_scale_columns(b, row):
            for g in range(PAGES):
                vs_cols[b, g] = columns(
                    lambda r: row[:, g * PAGE + r : (g + 1) * PAGE : PACK], f"vs_cols{b}{g}", 1.0, ("score_bank", "spare_bank")[b], f"vs_cols{g}"
                )

        def weigh(b, g):
            flat = sb([P, PACK, NQ], BF16, f"w_flat{b}{g}")
            for r in range(PACK):
                nc.scalar.activation(flat[:, r, :], probs[b, g][:, r, :], ACT.Copy, scale=vs_cols[b, g][:, r : r + 1])
            woven[b, g] = sb([P, NQ, PACK], BF16, f"w_woven{b}{g}")
            nc.scalar.copy(
                woven[b, g][:].rearrange("p (c i) r -> p c r i", i=4),
                flat[:].rearrange("p r (c i) -> p c r i", i=4),
            )

        def gather_values(first, count, tag):
            codes = sb([P, count * DV], U32, f"v_codes{first}", tag=tag)
            nc.vector.tensor_copy(codes[:], v_word_pool[:].bitcast(U32).indirect(listed(vcols, first * DV, count * DV)))
            return [codes[:, n * DV : (n + 1) * DV] for n in range(count)]

        inverse = {}

        def row_sums(b):
            total = sb([P, 1], F32, f"total{b}")
            nc.scalar.activation(total[:], sums[b, 0][:], ACT.Identity, bias=sums[b, 1][:], scale=1.0)
            inverse[b] = sb([P, 1], F32, f"inverse{b}")
            nc.vector.reciprocal(inverse[b][:], total[:])

        def multiply(b, g, acc, v_codes):
            w_codes = sb([P, NQ], U32, f"w_codes{b}{g}")
            w_bytes = sb([P, NQ], U8, f"w_bytes{b}{g}")
            nc.vector.quantize_mx(
                out=w_codes[:].bitcast(FP8X4), scales=w_bytes[:], in_=woven[b, g][:].rearrange("p q r -> p (q r)")
            )
            nc.tensor.matmul_mx(
                out=acc,
                lhsT=w_codes[:].bitcast(FP8X4),
                lhsT_scale=w_bytes[:],
                rhs=v_codes.bitcast(FP8X4),
                rhs_scale=v_bytes[:, (b * PAGES + g) * DV : (b * PAGES + g + 1) * DV],
                start=(g == 0),
                stop=(g == PAGES - 1),
            )

        def finish(b, acc):
            result = sb([P, DV], F32, f"result{b}", tag=f"w_flat1{1 - b}")
            nc.scalar.activation(result[:], acc, ACT.Copy, scale=inverse[b][:])
            nc.sync.dma_start(out[b], result[:])

        gather_key_bytes()
        nc.vector.quantize_mx(
            out=q_codes[:].bitcast(FP8X4), scales=q_bytes[:], in_=q_woven[:].rearrange("p b q j -> p (b q j)")
        )
        vs_pool = sb([P, T], F32, "vs_pool", tag="q_raw")
        nc.sync.dma_start(vs_pool[:], vs)
        v_word_pool = sb([P, POOL_PAGES * DV], I32, "v_word_pool", tag="q_woven")
        nc.sync.dma_start(
            v_word_pool[:].rearrange("p (u e) -> p u e", u=POOL_PAGES),
            v_words.rearrange("u p e r -> p u (e r)").bitcast(I32),
        )
        for j in range(4):
            nc.sync.dma_start(
                v_byte_pool[j:P:32, :].bitcast(I32).rearrange("f (u e) -> f u e", u=POOL_PAGES),
                v_scales[:, j:16:4, :].rearrange("u f e -> f u e").bitcast(I32),
            )

        for b in range(B):
            gather_bias(b)
        k_codes = sb([P, B * PAGES, PAGE], U32, "k_codes", tag="kb_row0")
        for b in range(B):
            for g in range(PAGES):
                scores(b, g)
        for g in range(PAGES):
            row_maximum(0, g)
        for g in range(PAGES):
            exponentials(0, g)
        row_sums(0)
        token_scale_columns(0, gather_token_scales(0))
        for g in range(PAGES):
            row_maximum(1, g)
        for g in range(PAGES):
            exponentials(1, g)
        row_sums(1)
        vs_row = gather_token_scales(1)
        for g in range(PAGES):
            weigh(0, g)
        token_scale_columns(1, vs_row)
        for g in range(PAGES):
            weigh(1, g)
        v_bytes = sb([P, B * PAGES * DV], U8, "v_bytes", tag="neg_c10")
        nc.vector.tensor_copy(v_bytes[:], v_byte_pool[:].indirect(vcols[:]))
        accs = [bank("turn_bank")[:].rearrange("q j s -> q (j s)")[:, :DV] for b in range(B)]
        for g, v_codes in enumerate(gather_values(0, PAGES, "neg_c11")):
            multiply(0, g, accs[0], v_codes)
        for g, tag in enumerate(("w_flat01", "w_flat10")):
            multiply(1, g, accs[1], gather_values(PAGES + g, 1, tag)[0])
        for b in range(B):
            finish(b, accs[b])
